import numpy as np
import ml_dtypes


def mxq(x, axis, fmt="e4m3"):
    dtype, down = {"e4m3": (ml_dtypes.float8_e4m3fn, 7), "e5m2": (ml_dtypes.float8_e5m2, 14)}[fmt]
    v = np.moveaxis(np.asarray(x, np.float32).astype(ml_dtypes.bfloat16).astype(np.float64), axis, -1)
    blocks = v.reshape(v.shape[:-1] + (-1, 32))
    amax = np.abs(blocks).max(-1, keepdims=True)
    byte = np.maximum(np.where(amax > 0, np.frexp(amax)[1] - 1 + 127, 0) - down, 1)
    scale = np.exp2(byte - 127.0)
    codes = (blocks / scale).astype(np.float32).astype(dtype).astype(np.float64)
    return np.moveaxis((codes * scale).reshape(v.shape), -1, axis)


WIDE = False


def mx_kscale(k, group=512):
    if not WIDE:
        return np.ones(k)
    levels = np.array([10, -10, 5, -5, 0])
    if group != 512:
        return np.exp2(np.random.permutation(np.resize(levels, k // group))).repeat(group)
    if k % 512:
        return np.exp2(np.random.permutation(np.resize(levels, k // 32))).repeat(32)
    a = np.empty((k // 512, 16))
    for p in range(k // 512):
        a[p, :8] = np.random.permutation(np.resize(levels, 8))
        for g in range(8):
            far = levels[np.abs(levels - a[p, g]) >= 10]
            a[p, g + 8] = far[np.random.randint(len(far))]
    return np.exp2(a.ravel()).repeat(32)


def f64(x):
    return np.asarray(x).astype(np.float64)


def silu(v):
    return v / (1.0 + np.exp(-v))


G, D, K, M, N = 2, 256, 512, 256, 512


def setup_inputs():
    n = np.random.standard_normal
    s = mx_kscale(D, 0)[:, None]
    u = mx_kscale(K)[:, None]
    return {
        "x": (n((G, D, N)) * s).astype(np.float32),
        "w1": (n((G, D, K)) / np.sqrt(D) / s).astype(np.float32),
        "hs": (np.random.uniform(0.5, 2.0, (G, K, 1)) * u).astype(np.float32),
        "w2": (n((G, K, M)) / np.sqrt(K) / u).astype(np.float32),
        "r": n((G, M, N)).astype(np.float32),
    }


def reference(x, w1, hs, w2, r):
    xq = mxq(f64(x), 1, "e4m3")
    h = mxq(f64(w1), 1, "e4m3").transpose(0, 2, 1) @ xq
    h = (silu(h)) * f64(hs)
    y = mxq(f64(w2), 1, "e4m3").transpose(0, 2, 1) @ mxq(h, 1, "e4m3")
    y = y + f64(r)
    return y

@@ -1,0 +1,226 @@
+from contextlib import ExitStack
+
+import concourse.mybir as mybir
+
+G, D, K, M, N = 2, 256, 512, 256, 512
+FLOPS = 2 * G * N * (D * K + K * M)
+
+F32 = mybir.dt.float32
+BF16 = mybir.dt.bfloat16
+U32 = mybir.dt.uint32
+U8 = mybir.dt.uint8
+FP8X4 = mybir.dt.float8_e4m3fn_x4
+ACT = mybir.ActivationFunctionType
+ALU = mybir.AluOpType
+
+P = 128
+PACK = 4
+ROWS = D // PACK
+CH = 128
+HALF = N // 2
+W1_VECTOR = 84
+
+
+def tile_rows_gmlp_silu_res_kernel(tc, x, w1, hs, w2, r, out):
+    nc = tc.nc
+    with ExitStack() as ctx:
+        sb = ctx.enter_context(tc.tile_pool(name="sb", bufs=1))
+        ps = ctx.enter_context(tc.psum_pool(name="ps", bufs=1))
+        ctx.enter_context(tc.manual_schedule())
+
+        def sbt(name, shape, dtype):
+            return sb.tile(shape, dtype, name=name, align_bytes=64)
+
+        w1_raw = sbt("w1_raw", [P, PACK, K], F32)
+        x_raw = [sbt("x_raw%d" % h, [P, PACK, HALF], F32) for h in range(2)]
+        w2_raw = [sbt("w2_raw%d" % g, [P, PACK, M], F32) for g in range(G)]
+        r_sb = [sbt("r_sb%d" % g, [P, 2, N], F32) for g in range(G)]
+        hs_sb = sbt("hs_sb", [P, G, 8], F32)
+        w1_bf = sbt("w1_bf", [P, PACK, P, PACK], BF16)
+        w1_codes = sbt("w1_codes", [P, K], U32)
+        w1_scales = sbt("w1_scales", [P, K], U8)
+        x_bf = [sbt("x_bf%d" % c, [P, CH, PACK], BF16) for c in range(4)]
+        x_codes = [sbt("x_codes%d" % c, [P, CH], U32) for c in range(4)]
+        x_scales = [sbt("x_scales%d" % c, [P, CH], U8) for c in range(4)]
+        w2_bf = [sbt("w2_bf%d" % g, [P, 2, P, PACK], BF16) for g in range(G)]
+        w2_codes = [sbt("w2_codes%d" % g, [P, M], U32) for g in range(G)]
+        w2_scales = [sbt("w2_scales%d" % g, [P, M], U8) for g in range(G)]
+        units = [(0, 0), (0, 1), (1, 0), (1, 1), (0, 2), (0, 3), (1, 2), (1, 3)]
+        act = [sbt("act%d" % u, [P, CH, PACK], F32) for u in range(8)]
+        h_bf = [sbt("h_bf%d" % u, [P, CH, PACK], BF16) for u in range(8)]
+        h_codes = [sbt("h_codes%d" % u, [P, CH], U32) for u in range(8)]
+        h_scales = [sbt("h_scales%d" % u, [P, CH], U8) for u in range(8)]
+        res = [sbt("res%d" % g, [P, 2, N], F32) for g in range(G)]
+        warm = sbt("warm", [P, 8], F32)
+        warm_out = sbt("warm_out", [P, 8], F32)
+        z_bank = [[ps.tile([P, PACK, CH], F32, name="z%d_%d" % (g, b)) for b in range(2)] for g in range(G)]
+        y_bank = [ps.tile([P, PACK, CH], F32, name="y%d" % b) for b in range(4)]
+
+        x_rows = x.rearrange("g (p j) n -> (g p) j n", j=PACK)
+        r_rows = [r[g].rearrange("(q t) n -> q t n", t=2) for g in range(G)]
+        out_rows = [out[g].rearrange("(q t) n -> q t n", t=2) for g in range(G)]
+
+        nc.gpsimd.memset(warm[:], 0.0)
+        nc.scalar.activation(out=warm_out[:], in_=warm[:], func=ACT.Silu)
+
+        nc.sync.dma_start(out=w1_raw[:], in_=w1.rearrange("g (p j) k -> (g p) j k", j=PACK))
+        nc.sync.dma_start(out=x_raw[0][:], in_=x_rows[:, :, 0:HALF])
+        nc.sync.dma_start(out=w2_raw[0][:], in_=w2[0].rearrange("(p j) m -> p j m", j=PACK))
+        nc.sync.dma_start(out=hs_sb[:, :, 0:PACK], in_=hs.rearrange("g (p j) o -> p g (j o)", j=PACK))
+        nc.sync.dma_start(out=x_raw[1][:], in_=x_rows[:, :, HALF:N])
+        nc.sync.dma_start(out=r_sb[0][:], in_=r_rows[0])
+        nc.sync.dma_start(out=w2_raw[1][:], in_=w2[1].rearrange("(p j) m -> p j m", j=PACK))
+        nc.sync.dma_start(out=r_sb[1][:], in_=r_rows[1])
+
+        def copy_on(engine, dst, src):
+            if engine == "vector":
+                nc.vector.tensor_copy(out=dst, in_=src)
+            else:
+                nc.scalar.copy(out=dst, in_=src)
+
+        def pack_w1(engine, lo, hi):
+            dst = w1_bf[:].rearrange("p t m j -> p m j t")[:, lo:hi]
+            src = w1_raw[:].rearrange("p j (m t) -> p m j t", t=PACK)[:, lo:hi]
+            copy_on(engine, dst, src)
+
+        def pack_x(engine, c):
+            raw = x_raw[c // 2][:, :, (c % 2) * CH : (c % 2 + 1) * CH]
+            dst = x_bf[c][:].rearrange("p (a i) j -> p a j i", i=4)
+            copy_on(engine, dst, raw.rearrange("p j (a i) -> p a j i", i=4))
+
+        def pack_w2(engine, g):
+            dst = w2_bf[g][:].rearrange("p t (a b) j -> p a j b t", b=2)
+            src = w2_raw[g][:].rearrange("p j (a b t) -> p a j b t", b=2, t=2)
+            copy_on(engine, dst, src)
+
+        def quantize(codes, scales, packed):
+            nc.vector.quantize_mx(out=codes[:].bitcast(FP8X4), scales=scales[:], in_=packed)
+
+        def quant_x(c):
+            quantize(x_codes[c], x_scales[c], x_bf[c][:].rearrange("p n j -> p (n j)"))
+
+        def quant_w2(g):
+            quantize(w2_codes[g], w2_scales[g], w2_bf[g][:].rearrange("p t q j -> p (t q j)"))
+
+        def layer1_pass(u, t):
+            g, c = units[u]
+            rows = slice(g * ROWS, (g + 1) * ROWS)
+            cols = slice(t * P, (t + 1) * P)
+            nc.tensor.matmul_mx(
+                out=z_bank[g][c % 2][:, t, :],
+                lhsT=w1_codes[rows, cols].bitcast(FP8X4),
+                lhsT_scale=w1_scales[rows, cols],
+                rhs=x_codes[c][rows, :].bitcast(FP8X4),
+                rhs_scale=x_scales[c][rows, :],
+                start=True,
+                stop=True,
+            )
+
+        def layer1(*us):
+            for t in range(PACK):
+                for u in us:
+                    layer1_pass(u, t)
+
+        def silu(u):
+            g, c = units[u]
+            nc.scalar.activation(out=act[u][:], in_=z_bank[g][c % 2][:].rearrange("p t n -> p n t"), func=ACT.Silu)
+
+        def scale(u):
+            g, c = units[u]
+            nc.vector.tensor_tensor(
+                out=h_bf[u][:],
+                in0=act[u][:],
+                in1=hs_sb[:, g, 0:PACK].unsqueeze(1).to_broadcast([P, CH, PACK]),
+                op=ALU.mult,
+            )
+
+        def quant_h(u):
+            quantize(h_codes[u], h_scales[u], h_bf[u][:].rearrange("p n j -> p (n j)"))
+
+        def layer2(u):
+            g, c = units[u]
+            for t in range(2):
+                cols = slice(t * P, (t + 1) * P)
+                nc.tensor.matmul_mx(
+                    out=y_bank[u % 4][:, t, :],
+                    lhsT=w2_codes[g][:, cols].bitcast(FP8X4),
+                    lhsT_scale=w2_scales[g][:, cols],
+                    rhs=h_codes[u][:].bitcast(FP8X4),
+                    rhs_scale=h_scales[u][:],
+                    start=True,
+                    stop=True,
+                )
+
+        def add_residual(u):
+            g, c = units[u]
+            cols = slice(c * CH, (c + 1) * CH)
+            nc.vector.tensor_tensor(out=res[g][:, :, cols], in0=y_bank[u % 4][:, 0:2, :], in1=r_sb[g][:, :, cols], op=ALU.add)
+
+        def store(g, lo, hi):
+            nc.sync.dma_start(out=out_rows[g][:, :, lo:hi], in_=res[g][:, :, lo:hi])
+
+        pack_w1("vector", 0, W1_VECTOR)
+        pack_w1("scalar", W1_VECTOR, P)
+        quantize(w1_codes, w1_scales, w1_bf[:].rearrange("p t m j -> p (t m j)"))
+        pack_x("scalar", 0)
+        pack_x("vector", 1)
+        quant_x(0)
+        quant_x(1)
+        layer1(0)
+        layer1(1, 2)
+        layer1(3)
+        pack_w2("vector", 0)
+        silu(0)
+        silu(1)
+        silu(2)
+        pack_x("scalar", 2)
+        silu(3)
+        pack_x("scalar", 3)
+        scale(0)
+        quant_w2(0)
+        scale(1)
+        quant_h(0)
+        layer2(0)
+        scale(2)
+        quant_h(1)
+        quant_x(2)
+        layer1(4)
+        layer2(1)
+        silu(4)
+        pack_w2("scalar", 1)
+        add_residual(0)
+        scale(3)
+        quant_h(2)
+        quant_x(3)
+        layer1(5, 6)
+        layer1(7)
+        silu(5)
+        silu(6)
+        silu(7)
+        add_residual(1)
+        scale(4)
+        quant_h(3)
+        quant_h(4)
+        layer2(4)
+        quant_w2(1)
+        layer2(2)
+        layer2(3)
+        scale(5)
+        add_residual(4)
+        quant_h(5)
+        layer2(5)
+        scale(6)
+        add_residual(2)
+        quant_h(6)
+        layer2(6)
+        scale(7)
+        add_residual(5)
+        store(0, 0, N)
+        quant_h(7)
+        add_residual(3)
+        layer2(7)
+        store(1, 0, HALF)
+        add_residual(6)
+        store(1, HALF, HALF + CH)
+        add_residual(7)
+        store(1, HALF + CH, N)

@@ -46,15 +46,15 @@ def tile_rows_gmlp_silu_res_kernel(tc, x, w1, hs, w2, r, out):
         w2_codes = [sbt("w2_codes%d" % g, [P, M], U32) for g in range(G)]
         w2_scales = [sbt("w2_scales%d" % g, [P, M], U8) for g in range(G)]
         units = [(0, 0), (0, 1), (1, 0), (1, 1), (0, 2), (0, 3), (1, 2), (1, 3)]
-        act = [sbt("act%d" % u, [P, CH, PACK], F32) for u in range(8)]
-        h_bf = [sbt("h_bf%d" % u, [P, CH, PACK], BF16) for u in range(8)]
-        h_codes = [sbt("h_codes%d" % u, [P, CH], U32) for u in range(8)]
-        h_scales = [sbt("h_scales%d" % u, [P, CH], U8) for u in range(8)]
+        act = [sbt("act%d" % v, [P, HALF, PACK], F32) for v in range(4)]
+        h_bf = [sbt("h_bf%d" % v, [P, HALF, PACK], BF16) for v in range(4)]
+        h_codes = [sbt("h_codes%d" % v, [P, HALF], U32) for v in range(4)]
+        h_scales = [sbt("h_scales%d" % v, [P, HALF], U8) for v in range(4)]
         res = [sbt("res%d" % g, [P, 2, N], F32) for g in range(G)]
         warm = sbt("warm", [P, 8], F32)
         warm_out = sbt("warm_out", [P, 8], F32)
         z_bank = [[ps.tile([P, PACK, CH], F32, name="z%d_%d" % (g, b)) for b in range(2)] for g in range(G)]
-        y_bank = [ps.tile([P, PACK, CH], F32, name="y%d" % b) for b in range(4)]
+        y_bank = [ps.tile([P, 2, HALF], F32, name="y%d" % b) for b in range(4)]
 
         x_rows = x.rearrange("g (p j) n -> (g p) j n", j=PACK)
         r_rows = [r[g].rearrange("(q t) n -> q t n", t=2) for g in range(G)]
@@ -94,13 +94,18 @@ def tile_rows_gmlp_silu_res_kernel(tc, x, w1, hs, w2, r, out):
             copy_on(engine, dst, src)
 
         def quantize(codes, scales, packed):
-            nc.vector.quantize_mx(out=codes[:].bitcast(FP8X4), scales=scales[:], in_=packed)
+            nc.vector.quantize_mx(out=codes.bitcast(FP8X4), scales=scales, in_=packed)
+
+        def quant_w1():
+            for t in range(PACK):
+                cols = slice(t * P, (t + 1) * P)
+                quantize(w1_codes[:, cols], w1_scales[:, cols], w1_bf[:, t].rearrange("p m j -> p (m j)"))
 
         def quant_x(c):
-            quantize(x_codes[c], x_scales[c], x_bf[c][:].rearrange("p n j -> p (n j)"))
+            quantize(x_codes[c][:], x_scales[c][:], x_bf[c][:].rearrange("p n j -> p (n j)"))
 
         def quant_w2(g):
-            quantize(w2_codes[g], w2_scales[g], w2_bf[g][:].rearrange("p t q j -> p (t q j)"))
+            quantize(w2_codes[g][:], w2_scales[g][:], w2_bf[g][:].rearrange("p t q j -> p (t q j)"))
 
         def layer1_pass(u, t):
             g, c = units[u]
@@ -121,106 +126,107 @@ def tile_rows_gmlp_silu_res_kernel(tc, x, w1, hs, w2, r, out):
                 for u in us:
                     layer1_pass(u, t)
 
+        def span(u, count):
+            return slice((u % 2) * CH, (u % 2 + count) * CH)
+
         def silu(u):
             g, c = units[u]
-            nc.scalar.activation(out=act[u][:], in_=z_bank[g][c % 2][:].rearrange("p t n -> p n t"), func=ACT.Silu)
+            nc.scalar.activation(out=act[u // 2][:, span(u, 1), :], in_=z_bank[g][c % 2][:].rearrange("p t n -> p n t"), func=ACT.Silu)
 
-        def scale(u):
+        def scale(u, count=1):
             g, c = units[u]
             nc.vector.tensor_tensor(
-                out=h_bf[u][:],
-                in0=act[u][:],
-                in1=hs_sb[:, g, 0:PACK].unsqueeze(1).to_broadcast([P, CH, PACK]),
+                out=h_bf[u // 2][:, span(u, count), :],
+                in0=act[u // 2][:, span(u, count), :],
+                in1=hs_sb[:, g, 0:PACK].unsqueeze(1).to_broadcast([P, count * CH, PACK]),
                 op=ALU.mult,
             )
 
-        def quant_h(u):
-            quantize(h_codes[u], h_scales[u], h_bf[u][:].rearrange("p n j -> p (n j)"))
+        def quant_h(u, count=1):
+            cols = span(u, count)
+            quantize(h_codes[u // 2][:, cols], h_scales[u // 2][:, cols], h_bf[u // 2][:, cols, :].rearrange("p n j -> p (n j)"))
 
-        def layer2(u):
+        def layer2(u, bank):
             g, c = units[u]
             for t in range(2):
                 cols = slice(t * P, (t + 1) * P)
                 nc.tensor.matmul_mx(
-                    out=y_bank[u % 4][:, t, :],
+                    out=y_bank[bank][:, t, span(u, 1)],
                     lhsT=w2_codes[g][:, cols].bitcast(FP8X4),
                     lhsT_scale=w2_scales[g][:, cols],
-                    rhs=h_codes[u][:].bitcast(FP8X4),
-                    rhs_scale=h_scales[u][:],
+                    rhs=h_codes[u // 2][:, span(u, 1)].bitcast(FP8X4),
+                    rhs_scale=h_scales[u // 2][:, span(u, 1)],
                     start=True,
                     stop=True,
                 )
 
-        def add_residual(u):
+        def add_residual(u, bank, count=1):
             g, c = units[u]
-            cols = slice(c * CH, (c + 1) * CH)
-            nc.vector.tensor_tensor(out=res[g][:, :, cols], in0=y_bank[u % 4][:, 0:2, :], in1=r_sb[g][:, :, cols], op=ALU.add)
+            cols = slice(c * CH, (c + count) * CH)
+            nc.vector.tensor_tensor(out=res[g][:, :, cols], in0=y_bank[bank][:, :, span(u, count)], in1=r_sb[g][:, :, cols], op=ALU.add)
 
         def store(g, lo, hi):
             nc.sync.dma_start(out=out_rows[g][:, :, lo:hi], in_=res[g][:, :, lo:hi])
 
+
         pack_w1("vector", 0, W1_VECTOR)
         pack_w1("scalar", W1_VECTOR, P)
-        quantize(w1_codes, w1_scales, w1_bf[:].rearrange("p t m j -> p (t m j)"))
+        quant_w1()
         pack_x("scalar", 0)
         pack_x("vector", 1)
         quant_x(0)
-        quant_x(1)
         layer1(0)
-        layer1(1, 2)
+        quant_x(1)
+        layer1(1)
+        layer1(2)
         layer1(3)
         pack_w2("vector", 0)
         silu(0)
         silu(1)
-        silu(2)
-        pack_x("scalar", 2)
-        silu(3)
         pack_x("scalar", 3)
-        scale(0)
+        silu(2)
+        silu(3)
         quant_w2(0)
-        scale(1)
-        quant_h(0)
-        layer2(0)
-        scale(2)
-        quant_h(1)
+        pack_x("vector", 2)
+        scale(0)
         quant_x(2)
         layer1(4)
-        layer2(1)
-        silu(4)
-        pack_w2("scalar", 1)
-        add_residual(0)
-        scale(3)
-        quant_h(2)
+        scale(1)
         quant_x(3)
-        layer1(5, 6)
+        layer1(5)
+        quant_h(0, 2)
+        layer2(0, 0)
+        layer2(1, 0)
+        layer1(6)
         layer1(7)
+        silu(4)
         silu(5)
+        pack_w2("scalar", 1)
         silu(6)
         silu(7)
-        add_residual(1)
-        scale(4)
-        quant_h(3)
-        quant_h(4)
-        layer2(4)
+        scale(2)
+        scale(3)
+        add_residual(0, 0, 2)
+        store(0, 0, HALF)
+        quant_h(2, 2)
+        scale(4, 2)
         quant_w2(1)
-        layer2(2)
-        layer2(3)
-        scale(5)
-        add_residual(4)
-        quant_h(5)
-        layer2(5)
+        layer2(2, 1)
+        layer2(3, 1)
+        quant_h(4, 2)
+        layer2(4, 2)
+        layer2(5, 2)
         scale(6)
-        add_residual(2)
-        quant_h(6)
-        layer2(6)
-        scale(7)
-        add_residual(5)
-        store(0, 0, N)
-        quant_h(7)
-        add_residual(3)
-        layer2(7)
+        add_residual(2, 1, 2)
         store(1, 0, HALF)
-        add_residual(6)
+        quant_h(6)
+        layer2(6, 3)
+        scale(7)
+        add_residual(4, 2, 2)
+        store(0, HALF, N)
+        quant_h(7)
+        layer2(7, 0)
+        add_residual(6, 3)
         store(1, HALF, HALF + CH)
-        add_residual(7)
+        add_residual(7, 0)
         store(1, HALF + CH, N)

from contextlib import ExitStack

import concourse.mybir as mybir

G, D, K, M, N = 2, 256, 512, 256, 512
FLOPS = 2 * G * N * (D * K + K * M)

F32 = mybir.dt.float32
BF16 = mybir.dt.bfloat16
U32 = mybir.dt.uint32
U8 = mybir.dt.uint8
FP8X4 = mybir.dt.float8_e4m3fn_x4
ACT = mybir.ActivationFunctionType
ALU = mybir.AluOpType

P = 128
PACK = 4
ROWS = D // PACK
CH = 128
HALF = N // 2
W1_VECTOR = 84


def tile_rows_gmlp_silu_res_kernel(tc, x, w1, hs, w2, r, out):
    nc = tc.nc
    with ExitStack() as ctx:
        sb = ctx.enter_context(tc.tile_pool(name="sb", bufs=1))
        ps = ctx.enter_context(tc.psum_pool(name="ps", bufs=1))
        ctx.enter_context(tc.manual_schedule())

        def sbt(name, shape, dtype):
            return sb.tile(shape, dtype, name=name, align_bytes=64)

        w1_raw = sbt("w1_raw", [P, PACK, K], F32)
        x_raw = [sbt("x_raw%d" % h, [P, PACK, HALF], F32) for h in range(2)]
        w2_raw = [sbt("w2_raw%d" % g, [P, PACK, M], F32) for g in range(G)]
        r_sb = [sbt("r_sb%d" % g, [P, 2, N], F32) for g in range(G)]
        hs_sb = sbt("hs_sb", [P, G, 8], F32)
        w1_bf = sbt("w1_bf", [P, PACK, P, PACK], BF16)
        w1_codes = sbt("w1_codes", [P, K], U32)
        w1_scales = sbt("w1_scales", [P, K], U8)
        x_bf = [sbt("x_bf%d" % c, [P, CH, PACK], BF16) for c in range(4)]
        x_codes = [sbt("x_codes%d" % c, [P, CH], U32) for c in range(4)]
        x_scales = [sbt("x_scales%d" % c, [P, CH], U8) for c in range(4)]
        w2_bf = [sbt("w2_bf%d" % g, [P, 2, P, PACK], BF16) for g in range(G)]
        w2_codes = [sbt("w2_codes%d" % g, [P, M], U32) for g in range(G)]
        w2_scales = [sbt("w2_scales%d" % g, [P, M], U8) for g in range(G)]
        units = [(0, 0), (0, 1), (1, 0), (1, 1), (0, 2), (0, 3), (1, 2), (1, 3)]
        act = [sbt("act%d" % v, [P, HALF, PACK], F32) for v in range(4)]
        h_bf = [sbt("h_bf%d" % v, [P, HALF, PACK], BF16) for v in range(4)]
        h_codes = [sbt("h_codes%d" % v, [P, HALF], U32) for v in range(4)]
        h_scales = [sbt("h_scales%d" % v, [P, HALF], U8) for v in range(4)]
        res = [sbt("res%d" % g, [P, 2, N], F32) for g in range(G)]
        warm = sbt("warm", [P, 8], F32)
        warm_out = sbt("warm_out", [P, 8], F32)
        z_bank = [[ps.tile([P, PACK, CH], F32, name="z%d_%d" % (g, b)) for b in range(2)] for g in range(G)]
        y_bank = [ps.tile([P, 2, HALF], F32, name="y%d" % b) for b in range(4)]

        x_rows = x.rearrange("g (p j) n -> (g p) j n", j=PACK)
        r_rows = [r[g].rearrange("(q t) n -> q t n", t=2) for g in range(G)]
        out_rows = [out[g].rearrange("(q t) n -> q t n", t=2) for g in range(G)]

        nc.gpsimd.memset(warm[:], 0.0)
        nc.scalar.activation(out=warm_out[:], in_=warm[:], func=ACT.Silu)

        nc.sync.dma_start(out=w1_raw[:], in_=w1.rearrange("g (p j) k -> (g p) j k", j=PACK))
        nc.sync.dma_start(out=x_raw[0][:], in_=x_rows[:, :, 0:HALF])
        nc.sync.dma_start(out=w2_raw[0][:], in_=w2[0].rearrange("(p j) m -> p j m", j=PACK))
        nc.sync.dma_start(out=hs_sb[:, :, 0:PACK], in_=hs.rearrange("g (p j) o -> p g (j o)", j=PACK))
        nc.sync.dma_start(out=x_raw[1][:], in_=x_rows[:, :, HALF:N])
        nc.sync.dma_start(out=r_sb[0][:], in_=r_rows[0])
        nc.sync.dma_start(out=w2_raw[1][:], in_=w2[1].rearrange("(p j) m -> p j m", j=PACK))
        nc.sync.dma_start(out=r_sb[1][:], in_=r_rows[1])

        def copy_on(engine, dst, src):
            if engine == "vector":
                nc.vector.tensor_copy(out=dst, in_=src)
            else:
                nc.scalar.copy(out=dst, in_=src)

        def pack_w1(engine, lo, hi):
            dst = w1_bf[:].rearrange("p t m j -> p m j t")[:, lo:hi]
            src = w1_raw[:].rearrange("p j (m t) -> p m j t", t=PACK)[:, lo:hi]
            copy_on(engine, dst, src)

        def pack_x(engine, c):
            raw = x_raw[c // 2][:, :, (c % 2) * CH : (c % 2 + 1) * CH]
            dst = x_bf[c][:].rearrange("p (a i) j -> p a j i", i=4)
            copy_on(engine, dst, raw.rearrange("p j (a i) -> p a j i", i=4))

        def pack_w2(engine, g):
            dst = w2_bf[g][:].rearrange("p t (a b) j -> p a j b t", b=2)
            src = w2_raw[g][:].rearrange("p j (a b t) -> p a j b t", b=2, t=2)
            copy_on(engine, dst, src)

        def quantize(codes, scales, packed):
            nc.vector.quantize_mx(out=codes.bitcast(FP8X4), scales=scales, in_=packed)

        def quant_w1():
            for t in range(PACK):
                cols = slice(t * P, (t + 1) * P)
                quantize(w1_codes[:, cols], w1_scales[:, cols], w1_bf[:, t].rearrange("p m j -> p (m j)"))

        def quant_x(c):
            quantize(x_codes[c][:], x_scales[c][:], x_bf[c][:].rearrange("p n j -> p (n j)"))

        def quant_w2(g):
            quantize(w2_codes[g][:], w2_scales[g][:], w2_bf[g][:].rearrange("p t q j -> p (t q j)"))

        def layer1_pass(u, t):
            g, c = units[u]
            rows = slice(g * ROWS, (g + 1) * ROWS)
            cols = slice(t * P, (t + 1) * P)
            nc.tensor.matmul_mx(
                out=z_bank[g][c % 2][:, t, :],
                lhsT=w1_codes[rows, cols].bitcast(FP8X4),
                lhsT_scale=w1_scales[rows, cols],
                rhs=x_codes[c][rows, :].bitcast(FP8X4),
                rhs_scale=x_scales[c][rows, :],
                start=True,
                stop=True,
            )

        def layer1(*us):
            for t in range(PACK):
                for u in us:
                    layer1_pass(u, t)

        def span(u, count):
            return slice((u % 2) * CH, (u % 2 + count) * CH)

        def silu(u):
            g, c = units[u]
            nc.scalar.activation(out=act[u // 2][:, span(u, 1), :], in_=z_bank[g][c % 2][:].rearrange("p t n -> p n t"), func=ACT.Silu)

        def scale(u, count=1):
            g, c = units[u]
            nc.vector.tensor_tensor(
                out=h_bf[u // 2][:, span(u, count), :],
                in0=act[u // 2][:, span(u, count), :],
                in1=hs_sb[:, g, 0:PACK].unsqueeze(1).to_broadcast([P, count * CH, PACK]),
                op=ALU.mult,
            )

        def quant_h(u, count=1):
            cols = span(u, count)
            quantize(h_codes[u // 2][:, cols], h_scales[u // 2][:, cols], h_bf[u // 2][:, cols, :].rearrange("p n j -> p (n j)"))

        def layer2(u, bank):
            g, c = units[u]
            for t in range(2):
                cols = slice(t * P, (t + 1) * P)
                nc.tensor.matmul_mx(
                    out=y_bank[bank][:, t, span(u, 1)],
                    lhsT=w2_codes[g][:, cols].bitcast(FP8X4),
                    lhsT_scale=w2_scales[g][:, cols],
                    rhs=h_codes[u // 2][:, span(u, 1)].bitcast(FP8X4),
                    rhs_scale=h_scales[u // 2][:, span(u, 1)],
                    start=True,
                    stop=True,
                )

        def add_residual(u, bank, count=1):
            g, c = units[u]
            cols = slice(c * CH, (c + count) * CH)
            nc.vector.tensor_tensor(out=res[g][:, :, cols], in0=y_bank[bank][:, :, span(u, count)], in1=r_sb[g][:, :, cols], op=ALU.add)

        def store(g, lo, hi):
            nc.sync.dma_start(out=out_rows[g][:, :, lo:hi], in_=res[g][:, :, lo:hi])


        pack_w1("vector", 0, W1_VECTOR)
        pack_w1("scalar", W1_VECTOR, P)
        quant_w1()
        pack_x("scalar", 0)
        pack_x("vector", 1)
        quant_x(0)
        layer1(0)
        quant_x(1)
        layer1(1)
        layer1(2)
        layer1(3)
        pack_w2("vector", 0)
        silu(0)
        silu(1)
        pack_x("scalar", 3)
        silu(2)
        silu(3)
        quant_w2(0)
        pack_x("vector", 2)
        scale(0)
        quant_x(2)
        layer1(4)
        scale(1)
        quant_x(3)
        layer1(5)
        quant_h(0, 2)
        layer2(0, 0)
        layer2(1, 0)
        layer1(6)
        layer1(7)
        silu(4)
        silu(5)
        pack_w2("scalar", 1)
        silu(6)
        silu(7)
        scale(2)
        scale(3)
        add_residual(0, 0, 2)
        store(0, 0, HALF)
        quant_h(2, 2)
        scale(4, 2)
        quant_w2(1)
        layer2(2, 1)
        layer2(3, 1)
        quant_h(4, 2)
        layer2(4, 2)
        layer2(5, 2)
        scale(6)
        add_residual(2, 1, 2)
        store(1, 0, HALF)
        quant_h(6)
        layer2(6, 3)
        scale(7)
        add_residual(4, 2, 2)
        store(0, HALF, N)
        quant_h(7)
        layer2(7, 0)
        add_residual(6, 3)
        store(1, HALF, HALF + CH)
        add_residual(7, 0)
        store(1, HALF + CH, N)
